import numpy as np
import ml_dtypes


def mxq(x, axis, fmt="e4m3"):
    dtype, down = {"e4m3": (ml_dtypes.float8_e4m3fn, 7), "e5m2": (ml_dtypes.float8_e5m2, 14)}[fmt]
    v = np.moveaxis(np.asarray(x, np.float32).astype(ml_dtypes.bfloat16).astype(np.float64), axis, -1)
    blocks = v.reshape(v.shape[:-1] + (-1, 32))
    amax = np.abs(blocks).max(-1, keepdims=True)
    byte = np.maximum(np.where(amax > 0, np.frexp(amax)[1] - 1 + 127, 0) - down, 1)
    scale = np.exp2(byte - 127.0)
    codes = (blocks / scale).astype(np.float32).astype(dtype).astype(np.float64)
    return np.moveaxis((codes * scale).reshape(v.shape), -1, axis)


WIDE = False


def mx_kscale(k):
    if not WIDE:
        return np.ones(k)
    levels = np.array([10, -10, 5, -5, 0])
    if k % 512:
        return np.exp2(np.random.permutation(np.resize(levels, k // 32))).repeat(32)
    a = np.empty((k // 512, 16))
    for p in range(k // 512):
        a[p, :8] = np.random.permutation(np.resize(levels, 8))
        for g in range(8):
            far = levels[np.abs(levels - a[p, g]) >= 10]
            a[p, g + 8] = far[np.random.randint(len(far))]
    return np.exp2(a.ravel()).repeat(32)


def f64(x):
    return np.asarray(x).astype(np.float64)


def striped8(idx):
    return np.concatenate([x.reshape(-1, 16).T for x in idx]).astype(np.uint16)


def runs(offs, k):
    lists = np.stack([offs[16 * r : 16 * r + 16].T.reshape(-1) for r in range(8)]).astype(np.int64)
    return lists[np.arange(k) % 512 // 64]


def pack_weight(w):
    k, n = w.shape
    w = f64(np.asarray(w, np.float32).astype(ml_dtypes.bfloat16)).reshape(k // 32, 32, n)
    amax = np.abs(w).max(1)
    byte = np.clip(np.where(amax > 0, np.frexp(amax)[1] - 1 + 127 - 7, 1), 1, 254)
    scaled = (w * np.exp2(127.0 - byte)[:, None, :]).reshape(k, n).astype(np.float32)
    words = np.ascontiguousarray(scaled.reshape(k // 512, 128, 4, n).transpose(0, 1, 3, 2)).astype(ml_dtypes.float8_e4m3fn).view(np.uint8)
    return words, np.ascontiguousarray(byte.astype(np.uint8).reshape(k // 512, 16, n))


def unpack_weight(words, scales):
    g, p, n, _ = words.shape
    vals = np.ascontiguousarray(words).view(ml_dtypes.float8_e4m3fn).astype(np.float64) * np.repeat(np.exp2(scales.astype(np.float64) - 127.0), 8, axis=1)[..., None]
    return vals.transpose(0, 1, 3, 2).reshape(g * 512, n)


def gelu(v):
    return 0.5 * v * (1.0 + np.tanh(np.sqrt(2.0 / np.pi) * (v + 0.044715 * v**3)))


K, T, S, H, N = 1024, 2048, 512, 512, 128


def setup_inputs():
    n = np.random.standard_normal
    s = mx_kscale(K)[:, None]
    u = mx_kscale(H)
    packed_xT = pack_weight(n((K, T)) * s)
    return {
        "x_words": packed_xT[0],
        "x_scales": packed_xT[1],
        "w1": (n((K, H)) / np.sqrt(K) / s * u).astype(np.float32),
        "w2": (n((H, N)) / np.sqrt(H) / u[:, None]).astype(np.float32),
        "offs": striped8(np.stack([np.random.permutation(T)[:S] for _ in range(8)])),
    }


def reference(x_words, x_scales, w1, w2, offs):
    xq = unpack_weight(x_words, x_scales)[np.arange(K)[:, None], runs(offs, K)]
    h = gelu(mxq(f64(w1), 0, "e4m3").T @ xq)
    return mxq(f64(w2), 0, "e4m3").T @ mxq(h, 0, "e4m3")

@@ -1,0 +1,128 @@
+from contextlib import ExitStack
+
+import concourse.mybir as mybir
+
+K, T, S, H, N = 1024, 2048, 512, 512, 128
+FLOPS = 2 * K * H * S + 2 * H * N * S
+
+F32 = mybir.dt.float32
+BF16 = mybir.dt.bfloat16
+I32 = mybir.dt.int32
+U32 = mybir.dt.uint32
+U16 = mybir.dt.uint16
+U8 = mybir.dt.uint8
+FP8X4 = mybir.dt.float8_e4m3fn_x4
+GELU = mybir.ActivationFunctionType.Gelu_apprx_tanh
+
+P = 128
+PACK = 4
+PASSES = 2
+HALF = 256
+CHUNK = 128
+
+
+def tile_picked_phmlp_gelu_p_kernel(tc, x_words, x_scales, w1, w2, offs, out):
+    nc = tc.nc
+    with ExitStack() as ctx:
+        keep = ctx.enter_context(tc.tile_pool(name="keep", bufs=1))
+        psum = ctx.enter_context(tc.psum_pool(name="psum", bufs=1))
+
+        offsets = keep.tile([P, S // 16], U16, name="offsets")
+        nc.sync.dma_start(offsets[:], offs)
+
+        scale_table = keep.tile([P, T], U8, name="scale_table", align_bytes=64)
+        nc.vector.memset(scale_table[:].bitcast(I32), 0)
+        nc.scalar.dma_start(scale_table[0:P:4, :].bitcast(I32), x_scales.rearrange("z q c -> q z c").bitcast(I32))
+
+        w1_raw = [keep.tile([P, PACK, H], F32, name=f"w1_raw{z}") for z in range(PASSES)]
+        for z in range(PASSES):
+            nc.sync.dma_start(w1_raw[z][:], w1[512 * z : 512 * (z + 1), :].rearrange("(p j) c -> p j c", j=PACK))
+        word_table = [keep.tile([P, T], I32, name=f"word_table{z}", align_bytes=64) for z in range(PASSES)]
+        for z in range(PASSES):
+            nc.sync.dma_start(word_table[z][:], x_words[z].rearrange("p c r -> p (c r)").bitcast(I32))
+        w2_raw = keep.tile([P, PACK, N], F32, name="w2_raw")
+        nc.sync.dma_start(w2_raw[:], w2.rearrange("(p j) n -> p j n", j=PACK))
+
+        x_planes = keep.tile([P, PASSES, S], U8, name="x_planes", align_bytes=64)
+        nc.vector.memset(x_planes[:].rearrange("p z s -> p (z s)").bitcast(I32), 0)
+        picked_scales = keep.tile([P, S], U8, name="picked_scales", align_bytes=64)
+        nc.vector.tensor_copy(picked_scales[:], scale_table[:].indirect(offsets[:]))
+        for q in range(4):
+            nc.scalar.dma_start(
+                x_planes[32 * q : 32 * q + 4, :, :].bitcast(I32),
+                picked_scales[32 * q : 32 * q + 32 : 4, :].bitcast(I32),
+            )
+
+        w1_codes, w1_scales = [], []
+        for z in range(PASSES):
+            grouped = keep.tile([P, PACK, P, PACK], BF16, name=f"w1_grouped{z}", align_bytes=64)
+            dst = grouped[:].rearrange("p t m j -> p m j t")
+            src = w1_raw[z][:].rearrange("p j (m t) -> p m j t", t=PACK)
+            nc.scalar.copy(dst[:, 0:64], src[:, 0:64])
+            nc.vector.tensor_copy(dst[:, 64:128], src[:, 64:128])
+            codes = keep.tile([P, H], U32, name=f"w1_codes{z}", align_bytes=64)
+            scales = keep.tile([P, H], U8, name=f"w1_scales{z}", align_bytes=64)
+            nc.vector.quantize_mx(out=codes[:].bitcast(FP8X4), scales=scales[:], in_=grouped[:].rearrange("p t m j -> p (t m j)"))
+            w1_codes.append(codes)
+            w1_scales.append(scales)
+
+        picked = {}
+        for z in range(PASSES):
+            for u in range(S // HALF):
+                picked[z, u] = keep.tile([P, HALF], U32, name=f"picked{z}_{u}", align_bytes=64)
+                nc.vector.tensor_copy(picked[z, u][:], word_table[z][:].bitcast(U32).indirect(offsets[:, 16 * u : 16 * (u + 1)]))
+
+        w2_grouped = keep.tile([P, N, PACK], BF16, name="w2_grouped", align_bytes=64)
+        nc.vector.tensor_copy(w2_grouped[:], w2_raw[:].rearrange("p j n -> p n j"))
+        w2_codes = keep.tile([P, N], U32, name="w2_codes", align_bytes=64)
+        w2_scales = keep.tile([P, N], U8, name="w2_scales", align_bytes=64)
+        nc.vector.quantize_mx(out=w2_codes[:].bitcast(FP8X4), scales=w2_scales[:], in_=w2_grouped[:].rearrange("p n j -> p (n j)"))
+
+        chunks = S // CHUNK
+        pre = [psum.tile([P, PACK, CHUNK], F32, name=f"pre{c}") for c in range(chunks)]
+
+        def layer1(c, t, z, start, stop):
+            u, a = divmod(c * CHUNK, HALF)
+            nc.tensor.matmul_mx(
+                out=pre[c][:, t, :],
+                lhsT=w1_codes[z][:, t * P : (t + 1) * P].bitcast(FP8X4),
+                lhsT_scale=w1_scales[z][:, t * P : (t + 1) * P],
+                rhs=picked[z, u][:, a : a + CHUNK].bitcast(FP8X4),
+                rhs_scale=x_planes[:, z, c * CHUNK : (c + 1) * CHUNK],
+                start=start,
+                stop=stop,
+            )
+
+        for z in range(PASSES):
+            for c in range(chunks):
+                for t in range(PACK):
+                    layer1(c, t, z, z == 0 and t == 0, z == PASSES - 1 and t == PACK - 1)
+
+        acc = [psum.tile([P, CHUNK], F32, name=f"acc{c}") for c in range(chunks)]
+
+        def layer2(c):
+            hidden = keep.tile([P, CHUNK, PACK], BF16, name=f"hidden{c}", align_bytes=64)
+            nc.scalar.activation(hidden[:], pre[c][:].rearrange("p t n -> p n t"), GELU)
+            h_codes = keep.tile([P, CHUNK], U32, name=f"h_codes{c}", align_bytes=64)
+            h_scales = keep.tile([P, CHUNK], U8, name=f"h_scales{c}", align_bytes=64)
+            nc.vector.quantize_mx(out=h_codes[:].bitcast(FP8X4), scales=h_scales[:], in_=hidden[:].rearrange("p n t -> p (n t)"))
+            nc.tensor.matmul_mx(
+                out=acc[c][:],
+                lhsT=w2_codes[:].bitcast(FP8X4),
+                lhsT_scale=w2_scales[:],
+                rhs=h_codes[:].bitcast(FP8X4),
+                rhs_scale=h_scales[:],
+                start=True,
+                stop=True,
+            )
+
+        def store(c):
+            result = keep.tile([P, CHUNK], F32, name=f"result{c}")
+            nc.vector.tensor_copy(result[:], acc[c][:])
+            nc.sync.dma_start(out[:, c * CHUNK : (c + 1) * CHUNK], result[:])
+
+        for c in range(chunks):
+            layer2(c)
+            if c > 0:
+                store(c - 1)
+        store(chunks - 1)

@@ -28,30 +28,35 @@ def tile_picked_phmlp_gelu_p_kernel(tc, x_words, x_scales, w1, w2, offs, out):
         psum = ctx.enter_context(tc.psum_pool(name="psum", bufs=1))
 
         offsets = keep.tile([P, S // 16], U16, name="offsets")
-        nc.sync.dma_start(offsets[:], offs)
 
-        scale_table = keep.tile([P, T], U8, name="scale_table", align_bytes=64)
+        warm = keep.tile([P, 2], F32, name="warm")
+        nc.gpsimd.memset(warm[:, 0:1], 0.0)
+        nc.scalar.activation(warm[:, 1:2], warm[:, 0:1], GELU)
+
+        scale_table = keep.tile([P, T], U8, name="scale_table", tag="reused", align_bytes=64)
         nc.vector.memset(scale_table[:].bitcast(I32), 0)
-        nc.scalar.dma_start(scale_table[0:P:4, :].bitcast(I32), x_scales.rearrange("z q c -> q z c").bitcast(I32))
 
-        w1_raw = [keep.tile([P, PACK, H], F32, name=f"w1_raw{z}") for z in range(PASSES)]
-        for z in range(PASSES):
-            nc.sync.dma_start(w1_raw[z][:], w1[512 * z : 512 * (z + 1), :].rearrange("(p j) c -> p j c", j=PACK))
-        word_table = [keep.tile([P, T], I32, name=f"word_table{z}", align_bytes=64) for z in range(PASSES)]
-        for z in range(PASSES):
-            nc.sync.dma_start(word_table[z][:], x_words[z].rearrange("p c r -> p (c r)").bitcast(I32))
-        w2_raw = keep.tile([P, PACK, N], F32, name="w2_raw")
-        nc.sync.dma_start(w2_raw[:], w2.rearrange("(p j) n -> p j n", j=PACK))
+        w1_raw = [keep.tile([P, PACK, H], F32, name=f"w1_raw{z}", tag=f"raw{z}") for z in range(PASSES)]
+        w1_rows = [w1[512 * z : 512 * (z + 1), :].rearrange("(p j) c -> p j c", j=PACK) for z in range(PASSES)]
+        nc.sync.dma_start(w1_raw[0][:, 0:2, :], w1_rows[0][:, 0:2, :])
+        nc.sync.dma_start(offsets[:], offs)
+        nc.sync.dma_start(scale_table[0:P:4, :].bitcast(I32), x_scales.rearrange("z q c -> q z c").bitcast(I32))
+        nc.sync.dma_start(w1_raw[0][:, 2:4, :], w1_rows[0][:, 2:4, :])
+        nc.sync.dma_start(w1_raw[1][:], w1_rows[1])
+        word_table = [keep.tile([P, T], I32, name="word_table0", align_bytes=64)]
+        nc.sync.dma_start(word_table[0][:], x_words[0].rearrange("p c r -> p (c r)").bitcast(I32))
 
         x_planes = keep.tile([P, PASSES, S], U8, name="x_planes", align_bytes=64)
         nc.vector.memset(x_planes[:].rearrange("p z s -> p (z s)").bitcast(I32), 0)
         picked_scales = keep.tile([P, S], U8, name="picked_scales", align_bytes=64)
         nc.vector.tensor_copy(picked_scales[:], scale_table[:].indirect(offsets[:]))
         for q in range(4):
-            nc.scalar.dma_start(
+            nc.sync.dma_start(
                 x_planes[32 * q : 32 * q + 4, :, :].bitcast(I32),
                 picked_scales[32 * q : 32 * q + 32 : 4, :].bitcast(I32),
             )
+        word_table.append(keep.tile([P, T], I32, name="word_table1", tag="reused", align_bytes=64))
+        nc.sync.dma_start(word_table[1][:], x_words[1].rearrange("p c r -> p (c r)").bitcast(I32))
 
         w1_codes, w1_scales = [], []
         for z in range(PASSES):
@@ -65,6 +70,9 @@ def tile_picked_phmlp_gelu_p_kernel(tc, x_words, x_scales, w1, w2, offs, out):
             nc.vector.quantize_mx(out=codes[:].bitcast(FP8X4), scales=scales[:], in_=grouped[:].rearrange("p t m j -> p (t m j)"))
             w1_codes.append(codes)
             w1_scales.append(scales)
+
+        w2_raw = keep.tile([P, PACK, N], F32, name="w2_raw", tag="raw0")
+        nc.sync.dma_start(w2_raw[:], w2.rearrange("(p j) n -> p j n", j=PACK))
 
         picked = {}
         for z in range(PASSES):

@@ -19,6 +19,7 @@ PACK = 4
 PASSES = 2
 HALF = 256
 CHUNK = 128
+SCALAR_SHARE = 44
 
 
 def tile_picked_phmlp_gelu_p_kernel(tc, x_words, x_scales, w1, w2, offs, out):
@@ -42,9 +43,10 @@ def tile_picked_phmlp_gelu_p_kernel(tc, x_words, x_scales, w1, w2, offs, out):
         nc.sync.dma_start(offsets[:], offs)
         nc.sync.dma_start(scale_table[0:P:4, :].bitcast(I32), x_scales.rearrange("z q c -> q z c").bitcast(I32))
         nc.sync.dma_start(w1_raw[0][:, 2:4, :], w1_rows[0][:, 2:4, :])
-        nc.sync.dma_start(w1_raw[1][:], w1_rows[1])
         word_table = [keep.tile([P, T], I32, name="word_table0", align_bytes=64)]
         nc.sync.dma_start(word_table[0][:], x_words[0].rearrange("p c r -> p (c r)").bitcast(I32))
+
+        nc.sync.dma_start(w1_raw[1][:], w1_rows[1])
 
         x_planes = keep.tile([P, PASSES, S], U8, name="x_planes", align_bytes=64)
         nc.vector.memset(x_planes[:].rearrange("p z s -> p (z s)").bitcast(I32), 0)
@@ -58,30 +60,38 @@ def tile_picked_phmlp_gelu_p_kernel(tc, x_words, x_scales, w1, w2, offs, out):
         word_table.append(keep.tile([P, T], I32, name="word_table1", tag="reused", align_bytes=64))
         nc.sync.dma_start(word_table[1][:], x_words[1].rearrange("p c r -> p (c r)").bitcast(I32))
 
-        w1_codes, w1_scales = [], []
-        for z in range(PASSES):
+        w1_codes, w1_scales, picked = {}, {}, {}
+
+        def quantize_w1(z):
             grouped = keep.tile([P, PACK, P, PACK], BF16, name=f"w1_grouped{z}", align_bytes=64)
             dst = grouped[:].rearrange("p t m j -> p m j t")
             src = w1_raw[z][:].rearrange("p j (m t) -> p m j t", t=PACK)
-            nc.scalar.copy(dst[:, 0:64], src[:, 0:64])
-            nc.vector.tensor_copy(dst[:, 64:128], src[:, 64:128])
-            codes = keep.tile([P, H], U32, name=f"w1_codes{z}", align_bytes=64)
-            scales = keep.tile([P, H], U8, name=f"w1_scales{z}", align_bytes=64)
-            nc.vector.quantize_mx(out=codes[:].bitcast(FP8X4), scales=scales[:], in_=grouped[:].rearrange("p t m j -> p (t m j)"))
-            w1_codes.append(codes)
-            w1_scales.append(scales)
+            nc.scalar.copy(dst[:, 0:SCALAR_SHARE], src[:, 0:SCALAR_SHARE])
+            nc.vector.tensor_copy(dst[:, SCALAR_SHARE:P], src[:, SCALAR_SHARE:P])
+            w1_codes[z] = keep.tile([P, H], U32, name=f"w1_codes{z}", align_bytes=64)
+            w1_scales[z] = keep.tile([P, H], U8, name=f"w1_scales{z}", align_bytes=64)
+            nc.vector.quantize_mx(
+                out=w1_codes[z][:].bitcast(FP8X4),
+                scales=w1_scales[z][:],
+                in_=grouped[:].rearrange("p t m j -> p (t m j)"),
+            )
 
-        w2_raw = keep.tile([P, PACK, N], F32, name="w2_raw", tag="raw0")
-        nc.sync.dma_start(w2_raw[:], w2.rearrange("(p j) n -> p j n", j=PACK))
-
-        picked = {}
-        for z in range(PASSES):
+        def pick_words(z):
             for u in range(S // HALF):
                 picked[z, u] = keep.tile([P, HALF], U32, name=f"picked{z}_{u}", align_bytes=64)
                 nc.vector.tensor_copy(picked[z, u][:], word_table[z][:].bitcast(U32).indirect(offsets[:, 16 * u : 16 * (u + 1)]))
 
+        quantize_w1(0)
+        w2_raw = keep.tile([P, PACK, N], F32, name="w2_raw", tag="raw0")
+        nc.sync.dma_start(w2_raw[:], w2.rearrange("(p j) n -> p j n", j=PACK))
+        pick_words(0)
+        quantize_w1(1)
+        pick_words(1)
+
         w2_grouped = keep.tile([P, N, PACK], BF16, name="w2_grouped", align_bytes=64)
-        nc.vector.tensor_copy(w2_grouped[:], w2_raw[:].rearrange("p j n -> p n j"))
+        nc.vector.tensor_copy(
+            w2_grouped[:].rearrange("p (c i) t -> p c t i", i=4), w2_raw[:].rearrange("p t (c i) -> p c t i", i=4)
+        )
         w2_codes = keep.tile([P, N], U32, name="w2_codes", align_bytes=64)
         w2_scales = keep.tile([P, N], U8, name="w2_scales", align_bytes=64)
         nc.vector.quantize_mx(out=w2_codes[:].bitcast(FP8X4), scales=w2_scales[:], in_=w2_grouped[:].rearrange("p n j -> p (n j)"))
@@ -109,7 +119,7 @@ def tile_picked_phmlp_gelu_p_kernel(tc, x_words, x_scales, w1, w2, offs, out):
         acc = [psum.tile([P, CHUNK], F32, name=f"acc{c}") for c in range(chunks)]
 
         def layer2(c):
-            hidden = keep.tile([P, CHUNK, PACK], BF16, name=f"hidden{c}", align_bytes=64)
+            hidden = keep.tile([P, CHUNK, PACK], BF16, name=f"hidden{c}", tag=f"hidden{c}", align_bytes=64)
             nc.scalar.activation(hidden[:], pre[c][:].rearrange("p t n -> p n t"), GELU)
             h_codes = keep.tile([P, CHUNK], U32, name=f"h_codes{c}", align_bytes=64)
             h_scales = keep.tile([P, CHUNK], U8, name=f"h_scales{c}", align_bytes=64)
@@ -125,7 +135,7 @@ def tile_picked_phmlp_gelu_p_kernel(tc, x_words, x_scales, w1, w2, offs, out):
             )
 
         def store(c):
-            result = keep.tile([P, CHUNK], F32, name=f"result{c}")
+            result = keep.tile([P, CHUNK], F32, name=f"result{c}", tag=f"hidden{c + 1}", align_bytes=64)
             nc.vector.tensor_copy(result[:], acc[c][:])
             nc.sync.dma_start(out[:, c * CHUNK : (c + 1) * CHUNK], result[:])
 

@@ -97,7 +97,7 @@ def tile_picked_phmlp_gelu_p_kernel(tc, x_words, x_scales, w1, w2, offs, out):
         nc.vector.quantize_mx(out=w2_codes[:].bitcast(FP8X4), scales=w2_scales[:], in_=w2_grouped[:].rearrange("p n j -> p (n j)"))
 
         chunks = S // CHUNK
-        pre = [psum.tile([P, PACK, CHUNK], F32, name=f"pre{c}") for c in range(chunks)]
+        pre = [psum.tile([P, PACK, CHUNK], F32, name=f"pre{c}", tag=f"pre{c}") for c in range(chunks)]
 
         def layer1(c, t, z, start, stop):
             u, a = divmod(c * CHUNK, HALF)
@@ -116,16 +116,20 @@ def tile_picked_phmlp_gelu_p_kernel(tc, x_words, x_scales, w1, w2, offs, out):
                 for t in range(PACK):
                     layer1(c, t, z, z == 0 and t == 0, z == PASSES - 1 and t == PACK - 1)
 
-        acc = [psum.tile([P, CHUNK], F32, name=f"acc{c}") for c in range(chunks)]
+        pieces = [(0, 128), (128, 128), (256, 128), (384, 64), (448, 64)]
+        acc = {}
 
-        def layer2(c):
-            hidden = keep.tile([P, CHUNK, PACK], BF16, name=f"hidden{c}", tag=f"hidden{c}", align_bytes=64)
-            nc.scalar.activation(hidden[:], pre[c][:].rearrange("p t n -> p n t"), GELU)
-            h_codes = keep.tile([P, CHUNK], U32, name=f"h_codes{c}", align_bytes=64)
-            h_scales = keep.tile([P, CHUNK], U8, name=f"h_scales{c}", align_bytes=64)
+        def layer2(i):
+            first, width = pieces[i]
+            c, a = divmod(first, CHUNK)
+            hidden = keep.tile([P, width, PACK], BF16, name=f"hidden{i}", tag=f"hidden{i}", align_bytes=64)
+            nc.scalar.activation(hidden[:], pre[c][:, :, a : a + width].rearrange("p t n -> p n t"), GELU, bias=warm[:, 1:2])
+            h_codes = keep.tile([P, width], U32, name=f"h_codes{i}", align_bytes=64)
+            h_scales = keep.tile([P, width], U8, name=f"h_scales{i}", align_bytes=64)
             nc.vector.quantize_mx(out=h_codes[:].bitcast(FP8X4), scales=h_scales[:], in_=hidden[:].rearrange("p n t -> p (n t)"))
+            acc[i] = psum.tile([P, width], F32, name=f"acc{i}", tag=f"acc{i}" if i < chunks else "pre0")
             nc.tensor.matmul_mx(
-                out=acc[c][:],
+                out=acc[i][:],
                 lhsT=w2_codes[:].bitcast(FP8X4),
                 lhsT_scale=w2_scales[:],
                 rhs=h_codes[:].bitcast(FP8X4),
@@ -134,13 +138,20 @@ def tile_picked_phmlp_gelu_p_kernel(tc, x_words, x_scales, w1, w2, offs, out):
                 stop=True,
             )
 
-        def store(c):
-            result = keep.tile([P, CHUNK], F32, name=f"result{c}", tag=f"hidden{c + 1}", align_bytes=64)
-            nc.vector.tensor_copy(result[:], acc[c][:])
-            nc.sync.dma_start(out[:, c * CHUNK : (c + 1) * CHUNK], result[:])
+        def store(i):
+            first, width = pieces[i]
+            result = keep.tile([P, width], F32, name=f"result{i}", tag=f"hidden{i + 1}", align_bytes=64)
+            nc.vector.tensor_copy(result[:], acc[i][:])
+            nc.sync.dma_start(out[:, first : first + width], result[:])
 
-        for c in range(chunks):
-            layer2(c)
-            if c > 0:
-                store(c - 1)
-        store(chunks - 1)
+        for i in range(len(pieces)):
+            layer2(i)
+            if 0 < i < 3:
+                store(i - 1)
+        late = keep.tile([P, 192], F32, name="late", align_bytes=64)
+        nc.scalar.copy(late[:, 0:128], acc[2][:])
+        nc.scalar.copy(late[:, 128:192], acc[3][:])
+        nc.sync.dma_start(out[:, 256:448], late[:])
+        last = keep.tile([P, 64], F32, name="last", align_bytes=64)
+        nc.vector.tensor_copy(last[:], acc[4][:])
+        nc.sync.dma_start(out[:, 448:512], last[:])

@@ -16,10 +16,16 @@ GELU = mybir.ActivationFunctionType.Gelu_apprx_tanh
 
 P = 128
 PACK = 4
-PASSES = 2
-HALF = 256
+K_PASS = P * PACK
+PASSES = K // K_PASS
+LIST_ROWS = 16
+QUADRANT = 32
+GATHER = 256
 CHUNK = 128
+CHUNKS = S // CHUNK
 SCALAR_SHARE = 44
+PIECES = [(0, CHUNK), (CHUNK, CHUNK), (2 * CHUNK, CHUNK), (3 * CHUNK, CHUNK // 2), (S - CHUNK // 2, CHUNK // 2)]
+CHUNK_ORDER = (0, 1, 3, 2)
 
 
 def tile_picked_phmlp_gelu_p_kernel(tc, x_words, x_scales, w1, w2, offs, out):
@@ -28,36 +34,35 @@ def tile_picked_phmlp_gelu_p_kernel(tc, x_words, x_scales, w1, w2, offs, out):
         keep = ctx.enter_context(tc.tile_pool(name="keep", bufs=1))
         psum = ctx.enter_context(tc.psum_pool(name="psum", bufs=1))
 
-        offsets = keep.tile([P, S // 16], U16, name="offsets")
+        offsets = keep.tile([P, S // LIST_ROWS], U16, name="offsets")
 
-        warm = keep.tile([P, 2], F32, name="warm")
-        nc.gpsimd.memset(warm[:, 0:1], 0.0)
-        nc.scalar.activation(warm[:, 1:2], warm[:, 0:1], GELU)
+        zero = keep.tile([P, 2], F32, name="zero")
+        nc.gpsimd.memset(zero[:, 0:1], 0.0)
+        nc.scalar.activation(zero[:, 1:2], zero[:, 0:1], GELU)
 
-        scale_table = keep.tile([P, T], U8, name="scale_table", tag="reused", align_bytes=64)
+        scale_table = keep.tile([P, T], U8, name="scale_table", tag="scales_then_words", align_bytes=64)
         nc.vector.memset(scale_table[:].bitcast(I32), 0)
 
         w1_raw = [keep.tile([P, PACK, H], F32, name=f"w1_raw{z}", tag=f"raw{z}") for z in range(PASSES)]
-        w1_rows = [w1[512 * z : 512 * (z + 1), :].rearrange("(p j) c -> p j c", j=PACK) for z in range(PASSES)]
+        w1_rows = [w1[K_PASS * z : K_PASS * (z + 1), :].rearrange("(p j) c -> p j c", j=PACK) for z in range(PASSES)]
         nc.sync.dma_start(w1_raw[0][:, 0:2, :], w1_rows[0][:, 0:2, :])
         nc.sync.dma_start(offsets[:], offs)
         nc.sync.dma_start(scale_table[0:P:4, :].bitcast(I32), x_scales.rearrange("z q c -> q z c").bitcast(I32))
         nc.sync.dma_start(w1_raw[0][:, 2:4, :], w1_rows[0][:, 2:4, :])
         word_table = [keep.tile([P, T], I32, name="word_table0", align_bytes=64)]
         nc.sync.dma_start(word_table[0][:], x_words[0].rearrange("p c r -> p (c r)").bitcast(I32))
-
         nc.sync.dma_start(w1_raw[1][:], w1_rows[1])
 
         x_planes = keep.tile([P, PASSES, S], U8, name="x_planes", align_bytes=64)
         nc.vector.memset(x_planes[:].rearrange("p z s -> p (z s)").bitcast(I32), 0)
         picked_scales = keep.tile([P, S], U8, name="picked_scales", align_bytes=64)
         nc.vector.tensor_copy(picked_scales[:], scale_table[:].indirect(offsets[:]))
-        for q in range(4):
+        for first_row in range(0, P, QUADRANT):
             nc.sync.dma_start(
-                x_planes[32 * q : 32 * q + 4, :, :].bitcast(I32),
-                picked_scales[32 * q : 32 * q + 32 : 4, :].bitcast(I32),
+                x_planes[first_row : first_row + 4, :, :].bitcast(I32),
+                picked_scales[first_row : first_row + QUADRANT : 4, :].bitcast(I32),
             )
-        word_table.append(keep.tile([P, T], I32, name="word_table1", tag="reused", align_bytes=64))
+        word_table.append(keep.tile([P, T], I32, name="word_table1", tag="scales_then_words", align_bytes=64))
         nc.sync.dma_start(word_table[1][:], x_words[1].rearrange("p c r -> p (c r)").bitcast(I32))
 
         w1_codes, w1_scales, picked = {}, {}, {}
@@ -77,9 +82,11 @@ def tile_picked_phmlp_gelu_p_kernel(tc, x_words, x_scales, w1, w2, offs, out):
             )
 
         def pick_words(z):
-            for u in range(S // HALF):
-                picked[z, u] = keep.tile([P, HALF], U32, name=f"picked{z}_{u}", align_bytes=64)
-                nc.vector.tensor_copy(picked[z, u][:], word_table[z][:].bitcast(U32).indirect(offsets[:, 16 * u : 16 * (u + 1)]))
+            columns = GATHER // LIST_ROWS
+            for u in range(S // GATHER):
+                picked[z, u] = keep.tile([P, GATHER], U32, name=f"picked{z}_{u}", align_bytes=64)
+                entries = offsets[:, columns * u : columns * (u + 1)]
+                nc.vector.tensor_copy(picked[z, u][:], word_table[z][:].bitcast(U32).indirect(entries))
 
         quantize_w1(0)
         w2_raw = keep.tile([P, PACK, N], F32, name="w2_raw", tag="raw0")
@@ -96,38 +103,34 @@ def tile_picked_phmlp_gelu_p_kernel(tc, x_words, x_scales, w1, w2, offs, out):
         w2_scales = keep.tile([P, N], U8, name="w2_scales", align_bytes=64)
         nc.vector.quantize_mx(out=w2_codes[:].bitcast(FP8X4), scales=w2_scales[:], in_=w2_grouped[:].rearrange("p n j -> p (n j)"))
 
-        chunks = S // CHUNK
-        pre = [psum.tile([P, PACK, CHUNK], F32, name=f"pre{c}", tag=f"pre{c}") for c in range(chunks)]
-
-        def layer1(c, t, z, start, stop):
-            u, a = divmod(c * CHUNK, HALF)
-            nc.tensor.matmul_mx(
-                out=pre[c][:, t, :],
-                lhsT=w1_codes[z][:, t * P : (t + 1) * P].bitcast(FP8X4),
-                lhsT_scale=w1_scales[z][:, t * P : (t + 1) * P],
-                rhs=picked[z, u][:, a : a + CHUNK].bitcast(FP8X4),
-                rhs_scale=x_planes[:, z, c * CHUNK : (c + 1) * CHUNK],
-                start=start,
-                stop=stop,
-            )
-
+        pre = [psum.tile([P, PACK, CHUNK], F32, name=f"pre{c}", tag=f"pre{c}") for c in range(CHUNKS)]
         for z in range(PASSES):
-            for c in range(chunks):
+            for c in CHUNK_ORDER:
+                u, within = divmod(c * CHUNK, GATHER)
                 for t in range(PACK):
-                    layer1(c, t, z, z == 0 and t == 0, z == PASSES - 1 and t == PACK - 1)
+                    nc.tensor.matmul_mx(
+                        out=pre[c][:, t, :],
+                        lhsT=w1_codes[z][:, t * P : (t + 1) * P].bitcast(FP8X4),
+                        lhsT_scale=w1_scales[z][:, t * P : (t + 1) * P],
+                        rhs=picked[z, u][:, within : within + CHUNK].bitcast(FP8X4),
+                        rhs_scale=x_planes[:, z, c * CHUNK : (c + 1) * CHUNK],
+                        start=z == 0 and t == 0,
+                        stop=z == PASSES - 1 and t == PACK - 1,
+                    )
 
-        pieces = [(0, 128), (128, 128), (256, 128), (384, 64), (448, 64)]
         acc = {}
 
-        def layer2(i):
-            first, width = pieces[i]
-            c, a = divmod(first, CHUNK)
+        def second_layer(i):
+            first, width = PIECES[i]
+            c, within = divmod(first, CHUNK)
             hidden = keep.tile([P, width, PACK], BF16, name=f"hidden{i}", tag=f"hidden{i}", align_bytes=64)
-            nc.scalar.activation(hidden[:], pre[c][:, :, a : a + width].rearrange("p t n -> p n t"), GELU, bias=warm[:, 1:2])
+            nc.scalar.activation(
+                hidden[:], pre[c][:, :, within : within + width].rearrange("p t n -> p n t"), GELU, bias=zero[:, 1:2]
+            )
             h_codes = keep.tile([P, width], U32, name=f"h_codes{i}", align_bytes=64)
             h_scales = keep.tile([P, width], U8, name=f"h_scales{i}", align_bytes=64)
             nc.vector.quantize_mx(out=h_codes[:].bitcast(FP8X4), scales=h_scales[:], in_=hidden[:].rearrange("p n t -> p (n t)"))
-            acc[i] = psum.tile([P, width], F32, name=f"acc{i}", tag=f"acc{i}" if i < chunks else "pre0")
+            acc[i] = psum.tile([P, width], F32, name=f"acc{i}", tag=f"acc{i}" if i < CHUNKS else "pre0")
             nc.tensor.matmul_mx(
                 out=acc[i][:],
                 lhsT=w2_codes[:].bitcast(FP8X4),
@@ -138,20 +141,25 @@ def tile_picked_phmlp_gelu_p_kernel(tc, x_words, x_scales, w1, w2, offs, out):
                 stop=True,
             )
 
-        def store(i):
-            first, width = pieces[i]
+        def store_early(i):
+            first, width = PIECES[i]
             result = keep.tile([P, width], F32, name=f"result{i}", tag=f"hidden{i + 1}", align_bytes=64)
             nc.vector.tensor_copy(result[:], acc[i][:])
             nc.sync.dma_start(out[:, first : first + width], result[:])
 
-        for i in range(len(pieces)):
-            layer2(i)
-            if 0 < i < 3:
-                store(i - 1)
-        late = keep.tile([P, 192], F32, name="late", align_bytes=64)
-        nc.scalar.copy(late[:, 0:128], acc[2][:])
-        nc.scalar.copy(late[:, 128:192], acc[3][:])
-        nc.sync.dma_start(out[:, 256:448], late[:])
-        last = keep.tile([P, 64], F32, name="last", align_bytes=64)
+        second_layer(0)
+        second_layer(1)
+        store_early(0)
+        second_layer(2)
+        store_early(1)
+        second_layer(3)
+        second_layer(4)
+
+        late_first, last_first = PIECES[2][0], PIECES[4][0]
+        late = keep.tile([P, last_first - late_first], F32, name="late", align_bytes=64)
+        nc.scalar.copy(late[:, 0:CHUNK], acc[2][:])
+        nc.scalar.copy(late[:, CHUNK : last_first - late_first], acc[3][:])
+        nc.sync.dma_start(out[:, late_first:last_first], late[:])
+        last = keep.tile([P, S - last_first], F32, name="last", align_bytes=64)
         nc.vector.tensor_copy(last[:], acc[4][:])
-        nc.sync.dma_start(out[:, 448:512], last[:])
+        nc.sync.dma_start(out[:, last_first:S], last[:])

@@ -25,7 +25,8 @@ CHUNK = 128
 CHUNKS = S // CHUNK
 SCALAR_SHARE = 44
 PIECES = [(0, CHUNK), (CHUNK, CHUNK), (2 * CHUNK, CHUNK), (3 * CHUNK, CHUNK // 2), (S - CHUNK // 2, CHUNK // 2)]
-CHUNK_ORDER = (0, 1, 3, 2)
+CHUNK_ORDER = (0, 1, 2, 3)
+WARM_UP = (512, 512, 128)
 
 
 def tile_picked_phmlp_gelu_p_kernel(tc, x_words, x_scales, w1, w2, offs, out):
@@ -49,9 +50,9 @@ def tile_picked_phmlp_gelu_p_kernel(tc, x_words, x_scales, w1, w2, offs, out):
         nc.sync.dma_start(offsets[:], offs)
         nc.sync.dma_start(scale_table[0:P:4, :].bitcast(I32), x_scales.rearrange("z q c -> q z c").bitcast(I32))
         nc.sync.dma_start(w1_raw[0][:, 2:4, :], w1_rows[0][:, 2:4, :])
+        nc.sync.dma_start(w1_raw[1][:], w1_rows[1])
         word_table = [keep.tile([P, T], I32, name="word_table0", align_bytes=64)]
         nc.sync.dma_start(word_table[0][:], x_words[0].rearrange("p c r -> p (c r)").bitcast(I32))
-        nc.sync.dma_start(w1_raw[1][:], w1_rows[1])
 
         x_planes = keep.tile([P, PASSES, S], U8, name="x_planes", align_bytes=64)
         nc.vector.memset(x_planes[:].rearrange("p z s -> p (z s)").bitcast(I32), 0)
@@ -91,8 +92,21 @@ def tile_picked_phmlp_gelu_p_kernel(tc, x_words, x_scales, w1, w2, offs, out):
         quantize_w1(0)
         w2_raw = keep.tile([P, PACK, N], F32, name="w2_raw", tag="raw0")
         nc.sync.dma_start(w2_raw[:], w2.rearrange("(p j) n -> p j n", j=PACK))
-        pick_words(0)
         quantize_w1(1)
+
+        for i, width in enumerate(WARM_UP):
+            unread = psum.tile([P, width], F32, name=f"unread{i}", tag=f"acc{i}")
+            nc.tensor.matmul_mx(
+                out=unread[:],
+                lhsT=w1_codes[1][:, 0:P].bitcast(FP8X4),
+                lhsT_scale=w1_scales[1][:, 0:P],
+                rhs=w1_codes[1][:, 0:width].bitcast(FP8X4),
+                rhs_scale=w1_scales[1][:, 0:width],
+                start=True,
+                stop=True,
+            )
+
+        pick_words(0)
         pick_words(1)
 
         w2_grouped = keep.tile([P, N, PACK], BF16, name="w2_grouped", align_bytes=64)

@@ -23,7 +23,7 @@ QUADRANT = 32
 GATHER = 256
 CHUNK = 128
 CHUNKS = S // CHUNK
-SCALAR_SHARE = 44
+SCALAR_SHARE = (96, 44)
 PIECES = [(0, CHUNK), (CHUNK, CHUNK), (2 * CHUNK, CHUNK), (3 * CHUNK, CHUNK // 2), (S - CHUNK // 2, CHUNK // 2)]
 CHUNK_ORDER = (0, 1, 2, 3)
 WARM_UP = (512, 512, 128)
@@ -33,6 +33,7 @@ def tile_picked_phmlp_gelu_p_kernel(tc, x_words, x_scales, w1, w2, offs, out):
     nc = tc.nc
     with ExitStack() as ctx:
         keep = ctx.enter_context(tc.tile_pool(name="keep", bufs=1))
+        reused = ctx.enter_context(tc.tile_pool(name="reused", bufs=1))
         psum = ctx.enter_context(tc.psum_pool(name="psum", bufs=1))
 
         offsets = keep.tile([P, S // LIST_ROWS], U16, name="offsets")
@@ -41,30 +42,34 @@ def tile_picked_phmlp_gelu_p_kernel(tc, x_words, x_scales, w1, w2, offs, out):
         nc.gpsimd.memset(zero[:, 0:1], 0.0)
         nc.scalar.activation(zero[:, 1:2], zero[:, 0:1], GELU)
 
-        scale_table = keep.tile([P, T], U8, name="scale_table", tag="scales_then_words", align_bytes=64)
+        scale_table = keep.tile([P, T], U8, name="scale_table", align_bytes=64)
         nc.vector.memset(scale_table[:].bitcast(I32), 0)
 
-        w1_raw = [keep.tile([P, PACK, H], F32, name=f"w1_raw{z}", tag=f"raw{z}") for z in range(PASSES)]
+        w1_raw = [
+            reused.tile([P, PACK, H], F32, name="w1_raw0", offset=0, align_bytes=64),
+            keep.tile([P, PACK, H], F32, name="w1_raw1", tag="raw1"),
+        ]
         w1_rows = [w1[K_PASS * z : K_PASS * (z + 1), :].rearrange("(p j) c -> p j c", j=PACK) for z in range(PASSES)]
-        nc.sync.dma_start(w1_raw[0][:, 0:2, :], w1_rows[0][:, 0:2, :])
+        nc.sync.dma_start(w1_raw[0][:], w1_rows[0])
         nc.sync.dma_start(offsets[:], offs)
         nc.sync.dma_start(scale_table[0:P:4, :].bitcast(I32), x_scales.rearrange("z q c -> q z c").bitcast(I32))
-        nc.sync.dma_start(w1_raw[0][:, 2:4, :], w1_rows[0][:, 2:4, :])
         nc.sync.dma_start(w1_raw[1][:], w1_rows[1])
         word_table = [keep.tile([P, T], I32, name="word_table0", align_bytes=64)]
         nc.sync.dma_start(word_table[0][:], x_words[0].rearrange("p c r -> p (c r)").bitcast(I32))
 
-        x_planes = keep.tile([P, PASSES, S], U8, name="x_planes", align_bytes=64)
-        nc.vector.memset(x_planes[:].rearrange("p z s -> p (z s)").bitcast(I32), 0)
         picked_scales = keep.tile([P, S], U8, name="picked_scales", align_bytes=64)
         nc.vector.tensor_copy(picked_scales[:], scale_table[:].indirect(offsets[:]))
-        for first_row in range(0, P, QUADRANT):
-            nc.sync.dma_start(
-                x_planes[first_row : first_row + 4, :, :].bitcast(I32),
-                picked_scales[first_row : first_row + QUADRANT : 4, :].bitcast(I32),
-            )
-        word_table.append(keep.tile([P, T], I32, name="word_table1", tag="scales_then_words", align_bytes=64))
-        nc.sync.dma_start(word_table[1][:], x_words[1].rearrange("p c r -> p (c r)").bitcast(I32))
+
+        def place_scales(plane, z):
+            nc.vector.tensor_copy(plane[:].bitcast(I32), picked_scales[:].bitcast(I32))
+            for r in range(1, 4):
+                nc.sync.dma_start(
+                    plane[4 * z + r : P : QUADRANT, :].bitcast(I32),
+                    picked_scales[4 * z + 8 * r : P : QUADRANT, :].bitcast(I32),
+                )
+
+        x_planes = [keep.tile([P, S], U8, name="x_plane0", align_bytes=64)]
+        place_scales(x_planes[0], 0)
 
         w1_codes, w1_scales, picked = {}, {}, {}
 
@@ -72,8 +77,9 @@ def tile_picked_phmlp_gelu_p_kernel(tc, x_words, x_scales, w1, w2, offs, out):
             grouped = keep.tile([P, PACK, P, PACK], BF16, name=f"w1_grouped{z}", align_bytes=64)
             dst = grouped[:].rearrange("p t m j -> p m j t")
             src = w1_raw[z][:].rearrange("p j (m t) -> p m j t", t=PACK)
-            nc.scalar.copy(dst[:, 0:SCALAR_SHARE], src[:, 0:SCALAR_SHARE])
-            nc.vector.tensor_copy(dst[:, SCALAR_SHARE:P], src[:, SCALAR_SHARE:P])
+            share = SCALAR_SHARE[z]
+            nc.scalar.copy(dst[:, 0:share], src[:, 0:share])
+            nc.vector.tensor_copy(dst[:, share:P], src[:, share:P])
             w1_codes[z] = keep.tile([P, H], U32, name=f"w1_codes{z}", align_bytes=64)
             w1_scales[z] = keep.tile([P, H], U8, name=f"w1_scales{z}", align_bytes=64)
             nc.vector.quantize_mx(
@@ -90,9 +96,13 @@ def tile_picked_phmlp_gelu_p_kernel(tc, x_words, x_scales, w1, w2, offs, out):
                 nc.vector.tensor_copy(picked[z, u][:], word_table[z][:].bitcast(U32).indirect(entries))
 
         quantize_w1(0)
-        w2_raw = keep.tile([P, PACK, N], F32, name="w2_raw", tag="raw0")
-        nc.sync.dma_start(w2_raw[:], w2.rearrange("(p j) n -> p j n", j=PACK))
+        word_table.append(reused.tile([P, T], I32, name="word_table1", offset=S, align_bytes=64))
+        nc.sync.dma_start(word_table[1][:], x_words[1].rearrange("p c r -> p (c r)").bitcast(I32))
+        x_planes.append(reused.tile([P, S], U8, name="x_plane1", offset=0, align_bytes=64))
+        place_scales(x_planes[1], 1)
         quantize_w1(1)
+        w2_raw = keep.tile([P, PACK, N], F32, name="w2_raw", tag="raw1")
+        nc.sync.dma_start(w2_raw[:], w2.rearrange("(p j) n -> p j n", j=PACK))
 
         for i, width in enumerate(WARM_UP):
             unread = psum.tile([P, width], F32, name=f"unread{i}", tag=f"acc{i}")
@@ -127,7 +137,7 @@ def tile_picked_phmlp_gelu_p_kernel(tc, x_words, x_scales, w1, w2, offs, out):
                         lhsT=w1_codes[z][:, t * P : (t + 1) * P].bitcast(FP8X4),
                         lhsT_scale=w1_scales[z][:, t * P : (t + 1) * P],
                         rhs=picked[z, u][:, within : within + CHUNK].bitcast(FP8X4),
-                        rhs_scale=x_planes[:, z, c * CHUNK : (c + 1) * CHUNK],
+                        rhs_scale=x_planes[z][4 * z : P, c * CHUNK : (c + 1) * CHUNK],
                         start=z == 0 and t == 0,
                         stop=z == PASSES - 1 and t == PACK - 1,
                     )
@@ -155,25 +165,21 @@ def tile_picked_phmlp_gelu_p_kernel(tc, x_words, x_scales, w1, w2, offs, out):
                 stop=True,
             )
 
-        def store_early(i):
-            first, width = PIECES[i]
-            result = keep.tile([P, width], F32, name=f"result{i}", tag=f"hidden{i + 1}", align_bytes=64)
-            nc.vector.tensor_copy(result[:], acc[i][:])
-            nc.sync.dma_start(out[:, first : first + width], result[:])
-
         second_layer(0)
         second_layer(1)
-        store_early(0)
+        early = keep.tile([P, CHUNK], F32, name="early", tag="hidden1", align_bytes=64)
+        nc.vector.tensor_copy(early[:], acc[0][:])
+        nc.sync.dma_start(out[:, 0:CHUNK], early[:])
         second_layer(2)
-        store_early(1)
+        last_first = PIECES[4][0]
+        late = keep.tile([P, last_first - CHUNK], F32, name="late", tag="hidden2", align_bytes=64)
+        nc.vector.tensor_copy(late[:, 0:CHUNK], acc[1][:])
         second_layer(3)
         second_layer(4)
 
-        late_first, last_first = PIECES[2][0], PIECES[4][0]
-        late = keep.tile([P, last_first - late_first], F32, name="late", align_bytes=64)
-        nc.scalar.copy(late[:, 0:CHUNK], acc[2][:])
-        nc.scalar.copy(late[:, CHUNK : last_first - late_first], acc[3][:])
-        nc.sync.dma_start(out[:, late_first:last_first], late[:])
+        nc.scalar.copy(late[:, CHUNK : 2 * CHUNK], acc[2][:])
+        nc.scalar.copy(late[:, 2 * CHUNK : last_first - CHUNK], acc[3][:])
+        nc.sync.dma_start(out[:, CHUNK:last_first], late[:])
         last = keep.tile([P, S - last_first], F32, name="last", align_bytes=64)
         nc.vector.tensor_copy(last[:], acc[4][:])
         nc.sync.dma_start(out[:, last_first:S], last[:])

@@ -26,6 +26,7 @@ CHUNKS = S // CHUNK
 SCALAR_SHARE = (96, 44)
 PIECES = [(0, CHUNK), (CHUNK, CHUNK), (2 * CHUNK, CHUNK), (3 * CHUNK, CHUNK // 2), (S - CHUNK // 2, CHUNK // 2)]
 CHUNK_ORDER = (0, 1, 2, 3)
+QUANTIZE = (H, H // 2)
 WARM_UP = (512, 512, 128)
 
 
@@ -82,11 +83,14 @@ def tile_picked_phmlp_gelu_p_kernel(tc, x_words, x_scales, w1, w2, offs, out):
             nc.vector.tensor_copy(dst[:, share:P], src[:, share:P])
             w1_codes[z] = keep.tile([P, H], U32, name=f"w1_codes{z}", align_bytes=64)
             w1_scales[z] = keep.tile([P, H], U8, name=f"w1_scales{z}", align_bytes=64)
-            nc.vector.quantize_mx(
-                out=w1_codes[z][:].bitcast(FP8X4),
-                scales=w1_scales[z][:],
-                in_=grouped[:].rearrange("p t m j -> p (t m j)"),
-            )
+            flat = grouped[:].rearrange("p t m j -> p (t m j)")
+            for first in range(0, H, QUANTIZE[z]):
+                words = slice(first, first + QUANTIZE[z])
+                nc.vector.quantize_mx(
+                    out=w1_codes[z][:, words].bitcast(FP8X4),
+                    scales=w1_scales[z][:, words],
+                    in_=flat[:, PACK * words.start : PACK * words.stop],
+                )
 
         def pick_words(z):
             columns = GATHER // LIST_ROWS
@@ -110,8 +114,8 @@ def tile_picked_phmlp_gelu_p_kernel(tc, x_words, x_scales, w1, w2, offs, out):
                 out=unread[:],
                 lhsT=w1_codes[1][:, 0:P].bitcast(FP8X4),
                 lhsT_scale=w1_scales[1][:, 0:P],
-                rhs=w1_codes[1][:, 0:width].bitcast(FP8X4),
-                rhs_scale=w1_scales[1][:, 0:width],
+                rhs=w1_codes[0][:, 0:width].bitcast(FP8X4),
+                rhs_scale=w1_scales[0][:, 0:width],
                 start=True,
                 stop=True,
             )

@@ -23,7 +23,7 @@ QUADRANT = 32
 GATHER = 256
 CHUNK = 128
 CHUNKS = S // CHUNK
-SCALAR_SHARE = (96, 44)
+SCALAR_SHARE = (112, 44)
 PIECES = [(0, CHUNK), (CHUNK, CHUNK), (2 * CHUNK, CHUNK), (3 * CHUNK, CHUNK // 2), (S - CHUNK // 2, CHUNK // 2)]
 CHUNK_ORDER = (0, 1, 2, 3)
 QUANTIZE = (H, H // 2)
@@ -34,7 +34,6 @@ def tile_picked_phmlp_gelu_p_kernel(tc, x_words, x_scales, w1, w2, offs, out):
     nc = tc.nc
     with ExitStack() as ctx:
         keep = ctx.enter_context(tc.tile_pool(name="keep", bufs=1))
-        reused = ctx.enter_context(tc.tile_pool(name="reused", bufs=1))
         psum = ctx.enter_context(tc.psum_pool(name="psum", bufs=1))
 
         offsets = keep.tile([P, S // LIST_ROWS], U16, name="offsets")
@@ -46,10 +45,7 @@ def tile_picked_phmlp_gelu_p_kernel(tc, x_words, x_scales, w1, w2, offs, out):
         scale_table = keep.tile([P, T], U8, name="scale_table", align_bytes=64)
         nc.vector.memset(scale_table[:].bitcast(I32), 0)
 
-        w1_raw = [
-            reused.tile([P, PACK, H], F32, name="w1_raw0", offset=0, align_bytes=64),
-            keep.tile([P, PACK, H], F32, name="w1_raw1", tag="raw1"),
-        ]
+        w1_raw = [keep.tile([P, PACK, H], F32, name=f"w1_raw{z}", tag=f"raw{z}") for z in range(PASSES)]
         w1_rows = [w1[K_PASS * z : K_PASS * (z + 1), :].rearrange("(p j) c -> p j c", j=PACK) for z in range(PASSES)]
         nc.sync.dma_start(w1_raw[0][:], w1_rows[0])
         nc.sync.dma_start(offsets[:], offs)
@@ -58,19 +54,23 @@ def tile_picked_phmlp_gelu_p_kernel(tc, x_words, x_scales, w1, w2, offs, out):
         word_table = [keep.tile([P, T], I32, name="word_table0", align_bytes=64)]
         nc.sync.dma_start(word_table[0][:], x_words[0].rearrange("p c r -> p (c r)").bitcast(I32))
 
-        picked_scales = keep.tile([P, S], U8, name="picked_scales", align_bytes=64)
+        picked_scales = keep.tile([P, S], U8, name="picked_scales", tag="scales_then_words", align_bytes=64)
         nc.vector.tensor_copy(picked_scales[:], scale_table[:].indirect(offsets[:]))
-
-        def place_scales(plane, z):
+        x_planes = [keep.tile([P, S], U8, name=f"x_plane{z}", align_bytes=64) for z in range(PASSES)]
+        for plane in x_planes:
             nc.vector.tensor_copy(plane[:].bitcast(I32), picked_scales[:].bitcast(I32))
+
+        def place_scales(z):
             for r in range(1, 4):
                 nc.sync.dma_start(
-                    plane[4 * z + r : P : QUADRANT, :].bitcast(I32),
-                    picked_scales[4 * z + 8 * r : P : QUADRANT, :].bitcast(I32),
+                    x_planes[z][4 * z + r : P : QUADRANT, :].bitcast(I32),
+                    x_planes[1 - z][4 * z + 8 * r : P : QUADRANT, :].bitcast(I32),
                 )
 
-        x_planes = [keep.tile([P, S], U8, name="x_plane0", align_bytes=64)]
-        place_scales(x_planes[0], 0)
+        place_scales(0)
+        word_table.append(keep.tile([P, T], I32, name="word_table1", tag="scales_then_words", align_bytes=64))
+        nc.sync.dma_start(word_table[1][:], x_words[1].rearrange("p c r -> p (c r)").bitcast(I32))
+        place_scales(1)
 
         w1_codes, w1_scales, picked = {}, {}, {}
 
@@ -100,10 +100,6 @@ def tile_picked_phmlp_gelu_p_kernel(tc, x_words, x_scales, w1, w2, offs, out):
                 nc.vector.tensor_copy(picked[z, u][:], word_table[z][:].bitcast(U32).indirect(entries))
 
         quantize_w1(0)
-        word_table.append(reused.tile([P, T], I32, name="word_table1", offset=S, align_bytes=64))
-        nc.sync.dma_start(word_table[1][:], x_words[1].rearrange("p c r -> p (c r)").bitcast(I32))
-        x_planes.append(reused.tile([P, S], U8, name="x_plane1", offset=0, align_bytes=64))
-        place_scales(x_planes[1], 1)
         quantize_w1(1)
         w2_raw = keep.tile([P, PACK, N], F32, name="w2_raw", tag="raw1")
         nc.sync.dma_start(w2_raw[:], w2.rearrange("(p j) n -> p j n", j=PACK))

@@ -26,8 +26,7 @@ CHUNKS = S // CHUNK
 SCALAR_SHARE = (112, 44)
 PIECES = [(0, CHUNK), (CHUNK, CHUNK), (2 * CHUNK, CHUNK), (3 * CHUNK, CHUNK // 2), (S - CHUNK // 2, CHUNK // 2)]
 CHUNK_ORDER = (0, 1, 2, 3)
-QUANTIZE = (H, H // 2)
-WARM_UP = (512, 512, 128)
+QUANTIZE = (H, H)
 
 
 def tile_picked_phmlp_gelu_p_kernel(tc, x_words, x_scales, w1, w2, offs, out):
@@ -50,9 +49,9 @@ def tile_picked_phmlp_gelu_p_kernel(tc, x_words, x_scales, w1, w2, offs, out):
         nc.sync.dma_start(w1_raw[0][:], w1_rows[0])
         nc.sync.dma_start(offsets[:], offs)
         nc.sync.dma_start(scale_table[0:P:4, :].bitcast(I32), x_scales.rearrange("z q c -> q z c").bitcast(I32))
-        nc.sync.dma_start(w1_raw[1][:], w1_rows[1])
         word_table = [keep.tile([P, T], I32, name="word_table0", align_bytes=64)]
         nc.sync.dma_start(word_table[0][:], x_words[0].rearrange("p c r -> p (c r)").bitcast(I32))
+        nc.sync.dma_start(w1_raw[1][:], w1_rows[1])
 
         picked_scales = keep.tile([P, S], U8, name="picked_scales", tag="scales_then_words", align_bytes=64)
         nc.vector.tensor_copy(picked_scales[:], scale_table[:].indirect(offsets[:]))
@@ -100,23 +99,11 @@ def tile_picked_phmlp_gelu_p_kernel(tc, x_words, x_scales, w1, w2, offs, out):
                 nc.vector.tensor_copy(picked[z, u][:], word_table[z][:].bitcast(U32).indirect(entries))
 
         quantize_w1(0)
+        pick_words(0)
         quantize_w1(1)
         w2_raw = keep.tile([P, PACK, N], F32, name="w2_raw", tag="raw1")
         nc.sync.dma_start(w2_raw[:], w2.rearrange("(p j) n -> p j n", j=PACK))
 
-        for i, width in enumerate(WARM_UP):
-            unread = psum.tile([P, width], F32, name=f"unread{i}", tag=f"acc{i}")
-            nc.tensor.matmul_mx(
-                out=unread[:],
-                lhsT=w1_codes[1][:, 0:P].bitcast(FP8X4),
-                lhsT_scale=w1_scales[1][:, 0:P],
-                rhs=w1_codes[0][:, 0:width].bitcast(FP8X4),
-                rhs_scale=w1_scales[0][:, 0:width],
-                start=True,
-                stop=True,
-            )
-
-        pick_words(0)
         pick_words(1)
 
         w2_grouped = keep.tile([P, N, PACK], BF16, name="w2_grouped", align_bytes=64)

@@ -15,6 +15,7 @@ FP8X4 = mybir.dt.float8_e4m3fn_x4
 GELU = mybir.ActivationFunctionType.Gelu_apprx_tanh
 
 P = 128
+ALIGN = 256
 PACK = 4
 K_PASS = P * PACK
 PASSES = K // K_PASS
@@ -35,27 +36,27 @@ def tile_picked_phmlp_gelu_p_kernel(tc, x_words, x_scales, w1, w2, offs, out):
         keep = ctx.enter_context(tc.tile_pool(name="keep", bufs=1))
         psum = ctx.enter_context(tc.psum_pool(name="psum", bufs=1))
 
-        offsets = keep.tile([P, S // LIST_ROWS], U16, name="offsets")
+        offsets = keep.tile([P, S // LIST_ROWS], U16, name="offsets", align_bytes=ALIGN)
 
         zero = keep.tile([P, 2], F32, name="zero")
         nc.gpsimd.memset(zero[:, 0:1], 0.0)
         nc.scalar.activation(zero[:, 1:2], zero[:, 0:1], GELU)
 
-        scale_table = keep.tile([P, T], U8, name="scale_table", align_bytes=64)
+        scale_table = keep.tile([P, T], U8, name="scale_table", align_bytes=ALIGN)
         nc.vector.memset(scale_table[:].bitcast(I32), 0)
 
-        w1_raw = [keep.tile([P, PACK, H], F32, name=f"w1_raw{z}", tag=f"raw{z}") for z in range(PASSES)]
+        w1_raw = [keep.tile([P, PACK, H], F32, name=f"w1_raw{z}", tag=f"raw{z}", align_bytes=ALIGN) for z in range(PASSES)]
         w1_rows = [w1[K_PASS * z : K_PASS * (z + 1), :].rearrange("(p j) c -> p j c", j=PACK) for z in range(PASSES)]
         nc.sync.dma_start(w1_raw[0][:], w1_rows[0])
         nc.sync.dma_start(offsets[:], offs)
         nc.sync.dma_start(scale_table[0:P:4, :].bitcast(I32), x_scales.rearrange("z q c -> q z c").bitcast(I32))
-        word_table = [keep.tile([P, T], I32, name="word_table0", align_bytes=64)]
+        word_table = [keep.tile([P, T], I32, name="word_table0", align_bytes=ALIGN)]
         nc.sync.dma_start(word_table[0][:], x_words[0].rearrange("p c r -> p (c r)").bitcast(I32))
         nc.sync.dma_start(w1_raw[1][:], w1_rows[1])
 
-        picked_scales = keep.tile([P, S], U8, name="picked_scales", tag="scales_then_words", align_bytes=64)
+        picked_scales = keep.tile([P, S], U8, name="picked_scales", tag="scales_then_words", align_bytes=ALIGN)
         nc.vector.tensor_copy(picked_scales[:], scale_table[:].indirect(offsets[:]))
-        x_planes = [keep.tile([P, S], U8, name=f"x_plane{z}", align_bytes=64) for z in range(PASSES)]
+        x_planes = [keep.tile([P, S], U8, name=f"x_plane{z}", align_bytes=ALIGN) for z in range(PASSES)]
         for plane in x_planes:
             nc.vector.tensor_copy(plane[:].bitcast(I32), picked_scales[:].bitcast(I32))
 
@@ -67,21 +68,21 @@ def tile_picked_phmlp_gelu_p_kernel(tc, x_words, x_scales, w1, w2, offs, out):
                 )
 
         place_scales(0)
-        word_table.append(keep.tile([P, T], I32, name="word_table1", tag="scales_then_words", align_bytes=64))
+        word_table.append(keep.tile([P, T], I32, name="word_table1", tag="scales_then_words", align_bytes=ALIGN))
         nc.sync.dma_start(word_table[1][:], x_words[1].rearrange("p c r -> p (c r)").bitcast(I32))
         place_scales(1)
 
         w1_codes, w1_scales, picked = {}, {}, {}
 
         def quantize_w1(z):
-            grouped = keep.tile([P, PACK, P, PACK], BF16, name=f"w1_grouped{z}", align_bytes=64)
+            grouped = keep.tile([P, PACK, P, PACK], BF16, name=f"w1_grouped{z}", align_bytes=ALIGN)
             dst = grouped[:].rearrange("p t m j -> p m j t")
             src = w1_raw[z][:].rearrange("p j (m t) -> p m j t", t=PACK)
             share = SCALAR_SHARE[z]
             nc.scalar.copy(dst[:, 0:share], src[:, 0:share])
             nc.vector.tensor_copy(dst[:, share:P], src[:, share:P])
-            w1_codes[z] = keep.tile([P, H], U32, name=f"w1_codes{z}", align_bytes=64)
-            w1_scales[z] = keep.tile([P, H], U8, name=f"w1_scales{z}", align_bytes=64)
+            w1_codes[z] = keep.tile([P, H], U32, name=f"w1_codes{z}", align_bytes=ALIGN)
+            w1_scales[z] = keep.tile([P, H], U8, name=f"w1_scales{z}", align_bytes=ALIGN)
             flat = grouped[:].rearrange("p t m j -> p (t m j)")
             for first in range(0, H, QUANTIZE[z]):
                 words = slice(first, first + QUANTIZE[z])
@@ -94,24 +95,24 @@ def tile_picked_phmlp_gelu_p_kernel(tc, x_words, x_scales, w1, w2, offs, out):
         def pick_words(z):
             columns = GATHER // LIST_ROWS
             for u in range(S // GATHER):
-                picked[z, u] = keep.tile([P, GATHER], U32, name=f"picked{z}_{u}", align_bytes=64)
+                picked[z, u] = keep.tile([P, GATHER], U32, name=f"picked{z}_{u}", align_bytes=ALIGN)
                 entries = offsets[:, columns * u : columns * (u + 1)]
                 nc.vector.tensor_copy(picked[z, u][:], word_table[z][:].bitcast(U32).indirect(entries))
 
         quantize_w1(0)
         pick_words(0)
         quantize_w1(1)
-        w2_raw = keep.tile([P, PACK, N], F32, name="w2_raw", tag="raw1")
+        w2_raw = keep.tile([P, PACK, N], F32, name="w2_raw", tag="raw1", align_bytes=ALIGN)
         nc.sync.dma_start(w2_raw[:], w2.rearrange("(p j) n -> p j n", j=PACK))
 
         pick_words(1)
 
-        w2_grouped = keep.tile([P, N, PACK], BF16, name="w2_grouped", align_bytes=64)
+        w2_grouped = keep.tile([P, N, PACK], BF16, name="w2_grouped", align_bytes=ALIGN)
         nc.vector.tensor_copy(
             w2_grouped[:].rearrange("p (c i) t -> p c t i", i=4), w2_raw[:].rearrange("p t (c i) -> p c t i", i=4)
         )
-        w2_codes = keep.tile([P, N], U32, name="w2_codes", align_bytes=64)
-        w2_scales = keep.tile([P, N], U8, name="w2_scales", align_bytes=64)
+        w2_codes = keep.tile([P, N], U32, name="w2_codes", align_bytes=ALIGN)
+        w2_scales = keep.tile([P, N], U8, name="w2_scales", align_bytes=ALIGN)
         nc.vector.quantize_mx(out=w2_codes[:].bitcast(FP8X4), scales=w2_scales[:], in_=w2_grouped[:].rearrange("p n j -> p (n j)"))
 
         pre = [psum.tile([P, PACK, CHUNK], F32, name=f"pre{c}", tag=f"pre{c}") for c in range(CHUNKS)]
@@ -134,12 +135,12 @@ def tile_picked_phmlp_gelu_p_kernel(tc, x_words, x_scales, w1, w2, offs, out):
         def second_layer(i):
             first, width = PIECES[i]
             c, within = divmod(first, CHUNK)
-            hidden = keep.tile([P, width, PACK], BF16, name=f"hidden{i}", tag=f"hidden{i}", align_bytes=64)
+            hidden = keep.tile([P, width, PACK], BF16, name=f"hidden{i}", tag=f"hidden{i}", align_bytes=ALIGN)
             nc.scalar.activation(
                 hidden[:], pre[c][:, :, within : within + width].rearrange("p t n -> p n t"), GELU, bias=zero[:, 1:2]
             )
-            h_codes = keep.tile([P, width], U32, name=f"h_codes{i}", align_bytes=64)
-            h_scales = keep.tile([P, width], U8, name=f"h_scales{i}", align_bytes=64)
+            h_codes = keep.tile([P, width], U32, name=f"h_codes{i}", align_bytes=ALIGN)
+            h_scales = keep.tile([P, width], U8, name=f"h_scales{i}", align_bytes=ALIGN)
             nc.vector.quantize_mx(out=h_codes[:].bitcast(FP8X4), scales=h_scales[:], in_=hidden[:].rearrange("p n t -> p (n t)"))
             acc[i] = psum.tile([P, width], F32, name=f"acc{i}", tag=f"acc{i}" if i < CHUNKS else "pre0")
             nc.tensor.matmul_mx(
@@ -154,12 +155,12 @@ def tile_picked_phmlp_gelu_p_kernel(tc, x_words, x_scales, w1, w2, offs, out):
 
         second_layer(0)
         second_layer(1)
-        early = keep.tile([P, CHUNK], F32, name="early", tag="hidden1", align_bytes=64)
+        early = keep.tile([P, CHUNK], F32, name="early", tag="hidden1", align_bytes=ALIGN)
         nc.vector.tensor_copy(early[:], acc[0][:])
         nc.sync.dma_start(out[:, 0:CHUNK], early[:])
         second_layer(2)
         last_first = PIECES[4][0]
-        late = keep.tile([P, last_first - CHUNK], F32, name="late", tag="hidden2", align_bytes=64)
+        late = keep.tile([P, last_first - CHUNK], F32, name="late", tag="hidden2", align_bytes=ALIGN)
         nc.vector.tensor_copy(late[:, 0:CHUNK], acc[1][:])
         second_layer(3)
         second_layer(4)
@@ -167,6 +168,6 @@ def tile_picked_phmlp_gelu_p_kernel(tc, x_words, x_scales, w1, w2, offs, out):
         nc.scalar.copy(late[:, CHUNK : 2 * CHUNK], acc[2][:])
         nc.scalar.copy(late[:, 2 * CHUNK : last_first - CHUNK], acc[3][:])
         nc.sync.dma_start(out[:, CHUNK:last_first], late[:])
-        last = keep.tile([P, S - last_first], F32, name="last", align_bytes=64)
+        last = keep.tile([P, S - last_first], F32, name="last", align_bytes=ALIGN)
         nc.vector.tensor_copy(last[:], acc[4][:])
         nc.sync.dma_start(out[:, last_first:S], last[:])

@@ -155,19 +155,17 @@ def tile_picked_phmlp_gelu_p_kernel(tc, x_words, x_scales, w1, w2, offs, out):
 
         second_layer(0)
         second_layer(1)
-        early = keep.tile([P, CHUNK], F32, name="early", tag="hidden1", align_bytes=ALIGN)
-        nc.vector.tensor_copy(early[:], acc[0][:])
-        nc.sync.dma_start(out[:, 0:CHUNK], early[:])
-        second_layer(2)
-        last_first = PIECES[4][0]
-        late = keep.tile([P, last_first - CHUNK], F32, name="late", tag="hidden2", align_bytes=ALIGN)
-        nc.vector.tensor_copy(late[:, 0:CHUNK], acc[1][:])
-        second_layer(3)
-        second_layer(4)
-
-        nc.scalar.copy(late[:, CHUNK : 2 * CHUNK], acc[2][:])
-        nc.scalar.copy(late[:, 2 * CHUNK : last_first - CHUNK], acc[3][:])
-        nc.sync.dma_start(out[:, CHUNK:last_first], late[:])
-        last = keep.tile([P, S - last_first], F32, name="last", align_bytes=ALIGN)
+        half = CHUNK // 2
+        early = keep.tile([P, 2 * CHUNK], F32, name="early", tag="hidden1", align_bytes=ALIGN)
+        nc.vector.tensor_copy(early[:, 0:CHUNK], acc[0][:])
+        for i in range(2, 5):
+            second_layer(i)
+        nc.scalar.copy(early[:, CHUNK : 2 * CHUNK], acc[1][:])
+        nc.sync.dma_start(out[:, 0 : 2 * CHUNK], early[:])
+        late = keep.tile([P, CHUNK + half], F32, name="late", align_bytes=ALIGN)
+        nc.scalar.copy(late[:, 0:CHUNK], acc[2][:])
+        nc.scalar.copy(late[:, CHUNK : CHUNK + half], acc[3][:])
+        nc.sync.dma_start(out[:, 2 * CHUNK : S - half], late[:])
+        last = keep.tile([P, half], F32, name="last", align_bytes=ALIGN)
         nc.vector.tensor_copy(last[:], acc[4][:])
-        nc.sync.dma_start(out[:, last_first:S], last[:])
+        nc.sync.dma_start(out[:, S - half : S], last[:])

@@ -156,10 +156,10 @@ def tile_picked_phmlp_gelu_p_kernel(tc, x_words, x_scales, w1, w2, offs, out):
         second_layer(0)
         second_layer(1)
         half = CHUNK // 2
-        early = keep.tile([P, 2 * CHUNK], F32, name="early", tag="hidden1", align_bytes=ALIGN)
-        nc.vector.tensor_copy(early[:, 0:CHUNK], acc[0][:])
         for i in range(2, 5):
             second_layer(i)
+        early = keep.tile([P, 2 * CHUNK], F32, name="early", align_bytes=ALIGN)
+        nc.scalar.copy(early[:, 0:CHUNK], acc[0][:])
         nc.scalar.copy(early[:, CHUNK : 2 * CHUNK], acc[1][:])
         nc.sync.dma_start(out[:, 0 : 2 * CHUNK], early[:])
         late = keep.tile([P, CHUNK + half], F32, name="late", align_bytes=ALIGN)

@@ -26,7 +26,8 @@ CHUNK = 128
 CHUNKS = S // CHUNK
 SCALAR_SHARE = (112, 44)
 PIECES = [(0, CHUNK), (CHUNK, CHUNK), (2 * CHUNK, CHUNK), (3 * CHUNK, CHUNK // 2), (S - CHUNK // 2, CHUNK // 2)]
-CHUNK_ORDER = (0, 1, 2, 3)
+FIRST_BANKS = (range(0, 1), range(1, 2), range(2, 4))
+FREE_BANKS = 8 - len(FIRST_BANKS) - (CHUNKS - 1)
 QUANTIZE = (H, H)
 
 
@@ -115,19 +116,20 @@ def tile_picked_phmlp_gelu_p_kernel(tc, x_words, x_scales, w1, w2, offs, out):
         w2_scales = keep.tile([P, N], U8, name="w2_scales", align_bytes=ALIGN)
         nc.vector.quantize_mx(out=w2_codes[:].bitcast(FP8X4), scales=w2_scales[:], in_=w2_grouped[:].rearrange("p n j -> p (n j)"))
 
-        pre = [psum.tile([P, PACK, CHUNK], F32, name=f"pre{c}", tag=f"pre{c}") for c in range(CHUNKS)]
+        banks = [(0, tiles) for tiles in FIRST_BANKS] + [(c, range(PACK)) for c in range(1, CHUNKS)]
+        pre = [psum.tile([P, len(tiles), CHUNK], F32, name=f"pre{b}", tag=f"pre{b}") for b, (c, tiles) in enumerate(banks)]
         for z in range(PASSES):
-            for c in CHUNK_ORDER:
+            for b, (c, tiles) in enumerate(banks):
                 u, within = divmod(c * CHUNK, GATHER)
-                for t in range(PACK):
+                for t in tiles:
                     nc.tensor.matmul_mx(
-                        out=pre[c][:, t, :],
+                        out=pre[b][:, t - tiles[0], :],
                         lhsT=w1_codes[z][:, t * P : (t + 1) * P].bitcast(FP8X4),
                         lhsT_scale=w1_scales[z][:, t * P : (t + 1) * P],
                         rhs=picked[z, u][:, within : within + CHUNK].bitcast(FP8X4),
                         rhs_scale=x_planes[z][4 * z : P, c * CHUNK : (c + 1) * CHUNK],
-                        start=z == 0 and t == 0,
-                        stop=z == PASSES - 1 and t == PACK - 1,
+                        start=z == 0 and t == tiles[0],
+                        stop=z == PASSES - 1 and t == tiles[-1],
                     )
 
         acc = {}
@@ -136,13 +138,22 @@ def tile_picked_phmlp_gelu_p_kernel(tc, x_words, x_scales, w1, w2, offs, out):
             first, width = PIECES[i]
             c, within = divmod(first, CHUNK)
             hidden = keep.tile([P, width, PACK], BF16, name=f"hidden{i}", tag=f"hidden{i}", align_bytes=ALIGN)
-            nc.scalar.activation(
-                hidden[:], pre[c][:, :, within : within + width].rearrange("p t n -> p n t"), GELU, bias=zero[:, 1:2]
-            )
+            if c == 0:
+                by_tile = keep.tile([P, PACK, CHUNK], BF16, name="by_tile", align_bytes=ALIGN)
+                for b, tiles in enumerate(FIRST_BANKS):
+                    nc.scalar.activation(by_tile[:, tiles[0] : tiles[-1] + 1, :], pre[b][:], GELU, bias=zero[:, 1:2])
+                nc.vector.tensor_copy(
+                    hidden[:].rearrange("p (c i) t -> p c t i", i=4), by_tile[:].rearrange("p t (c i) -> p c t i", i=4)
+                )
+            else:
+                bank = pre[len(FIRST_BANKS) - 1 + c]
+                nc.scalar.activation(
+                    hidden[:], bank[:, :, within : within + width].rearrange("p t n -> p n t"), GELU, bias=zero[:, 1:2]
+                )
             h_codes = keep.tile([P, width], U32, name=f"h_codes{i}", align_bytes=ALIGN)
             h_scales = keep.tile([P, width], U8, name=f"h_scales{i}", align_bytes=ALIGN)
             nc.vector.quantize_mx(out=h_codes[:].bitcast(FP8X4), scales=h_scales[:], in_=hidden[:].rearrange("p n t -> p (n t)"))
-            acc[i] = psum.tile([P, width], F32, name=f"acc{i}", tag=f"acc{i}" if i < CHUNKS else "pre0")
+            acc[i] = psum.tile([P, width], F32, name=f"acc{i}", tag=f"acc{i}" if i < FREE_BANKS else f"pre{i - FREE_BANKS}")
             nc.tensor.matmul_mx(
                 out=acc[i][:],
                 lhsT=w2_codes[:].bitcast(FP8X4),

from contextlib import ExitStack

import concourse.mybir as mybir

K, T, S, H, N = 1024, 2048, 512, 512, 128
FLOPS = 2 * K * H * S + 2 * H * N * S

F32 = mybir.dt.float32
BF16 = mybir.dt.bfloat16
I32 = mybir.dt.int32
U32 = mybir.dt.uint32
U16 = mybir.dt.uint16
U8 = mybir.dt.uint8
FP8X4 = mybir.dt.float8_e4m3fn_x4
GELU = mybir.ActivationFunctionType.Gelu_apprx_tanh

P = 128
ALIGN = 256
PACK = 4
K_PASS = P * PACK
PASSES = K // K_PASS
LIST_ROWS = 16
QUADRANT = 32
GATHER = 256
CHUNK = 128
CHUNKS = S // CHUNK
SCALAR_SHARE = (112, 44)
PIECES = [(0, CHUNK), (CHUNK, CHUNK), (2 * CHUNK, CHUNK), (3 * CHUNK, CHUNK // 2), (S - CHUNK // 2, CHUNK // 2)]
FIRST_BANKS = (range(0, 1), range(1, 2), range(2, 4))
FREE_BANKS = 8 - len(FIRST_BANKS) - (CHUNKS - 1)
QUANTIZE = (H, H)


def tile_picked_phmlp_gelu_p_kernel(tc, x_words, x_scales, w1, w2, offs, out):
    nc = tc.nc
    with ExitStack() as ctx:
        keep = ctx.enter_context(tc.tile_pool(name="keep", bufs=1))
        psum = ctx.enter_context(tc.psum_pool(name="psum", bufs=1))

        offsets = keep.tile([P, S // LIST_ROWS], U16, name="offsets", align_bytes=ALIGN)

        zero = keep.tile([P, 2], F32, name="zero")
        nc.gpsimd.memset(zero[:, 0:1], 0.0)
        nc.scalar.activation(zero[:, 1:2], zero[:, 0:1], GELU)

        scale_table = keep.tile([P, T], U8, name="scale_table", align_bytes=ALIGN)
        nc.vector.memset(scale_table[:].bitcast(I32), 0)

        w1_raw = [keep.tile([P, PACK, H], F32, name=f"w1_raw{z}", tag=f"raw{z}", align_bytes=ALIGN) for z in range(PASSES)]
        w1_rows = [w1[K_PASS * z : K_PASS * (z + 1), :].rearrange("(p j) c -> p j c", j=PACK) for z in range(PASSES)]
        nc.sync.dma_start(w1_raw[0][:], w1_rows[0])
        nc.sync.dma_start(offsets[:], offs)
        nc.sync.dma_start(scale_table[0:P:4, :].bitcast(I32), x_scales.rearrange("z q c -> q z c").bitcast(I32))
        word_table = [keep.tile([P, T], I32, name="word_table0", align_bytes=ALIGN)]
        nc.sync.dma_start(word_table[0][:], x_words[0].rearrange("p c r -> p (c r)").bitcast(I32))
        nc.sync.dma_start(w1_raw[1][:], w1_rows[1])

        picked_scales = keep.tile([P, S], U8, name="picked_scales", tag="scales_then_words", align_bytes=ALIGN)
        nc.vector.tensor_copy(picked_scales[:], scale_table[:].indirect(offsets[:]))
        x_planes = [keep.tile([P, S], U8, name=f"x_plane{z}", align_bytes=ALIGN) for z in range(PASSES)]
        for plane in x_planes:
            nc.vector.tensor_copy(plane[:].bitcast(I32), picked_scales[:].bitcast(I32))

        def place_scales(z):
            for r in range(1, 4):
                nc.sync.dma_start(
                    x_planes[z][4 * z + r : P : QUADRANT, :].bitcast(I32),
                    x_planes[1 - z][4 * z + 8 * r : P : QUADRANT, :].bitcast(I32),
                )

        place_scales(0)
        word_table.append(keep.tile([P, T], I32, name="word_table1", tag="scales_then_words", align_bytes=ALIGN))
        nc.sync.dma_start(word_table[1][:], x_words[1].rearrange("p c r -> p (c r)").bitcast(I32))
        place_scales(1)

        w1_codes, w1_scales, picked = {}, {}, {}

        def quantize_w1(z):
            grouped = keep.tile([P, PACK, P, PACK], BF16, name=f"w1_grouped{z}", align_bytes=ALIGN)
            dst = grouped[:].rearrange("p t m j -> p m j t")
            src = w1_raw[z][:].rearrange("p j (m t) -> p m j t", t=PACK)
            share = SCALAR_SHARE[z]
            nc.scalar.copy(dst[:, 0:share], src[:, 0:share])
            nc.vector.tensor_copy(dst[:, share:P], src[:, share:P])
            w1_codes[z] = keep.tile([P, H], U32, name=f"w1_codes{z}", align_bytes=ALIGN)
            w1_scales[z] = keep.tile([P, H], U8, name=f"w1_scales{z}", align_bytes=ALIGN)
            flat = grouped[:].rearrange("p t m j -> p (t m j)")
            for first in range(0, H, QUANTIZE[z]):
                words = slice(first, first + QUANTIZE[z])
                nc.vector.quantize_mx(
                    out=w1_codes[z][:, words].bitcast(FP8X4),
                    scales=w1_scales[z][:, words],
                    in_=flat[:, PACK * words.start : PACK * words.stop],
                )

        def pick_words(z):
            columns = GATHER // LIST_ROWS
            for u in range(S // GATHER):
                picked[z, u] = keep.tile([P, GATHER], U32, name=f"picked{z}_{u}", align_bytes=ALIGN)
                entries = offsets[:, columns * u : columns * (u + 1)]
                nc.vector.tensor_copy(picked[z, u][:], word_table[z][:].bitcast(U32).indirect(entries))

        quantize_w1(0)
        pick_words(0)
        quantize_w1(1)
        w2_raw = keep.tile([P, PACK, N], F32, name="w2_raw", tag="raw1", align_bytes=ALIGN)
        nc.sync.dma_start(w2_raw[:], w2.rearrange("(p j) n -> p j n", j=PACK))

        pick_words(1)

        w2_grouped = keep.tile([P, N, PACK], BF16, name="w2_grouped", align_bytes=ALIGN)
        nc.vector.tensor_copy(
            w2_grouped[:].rearrange("p (c i) t -> p c t i", i=4), w2_raw[:].rearrange("p t (c i) -> p c t i", i=4)
        )
        w2_codes = keep.tile([P, N], U32, name="w2_codes", align_bytes=ALIGN)
        w2_scales = keep.tile([P, N], U8, name="w2_scales", align_bytes=ALIGN)
        nc.vector.quantize_mx(out=w2_codes[:].bitcast(FP8X4), scales=w2_scales[:], in_=w2_grouped[:].rearrange("p n j -> p (n j)"))

        banks = [(0, tiles) for tiles in FIRST_BANKS] + [(c, range(PACK)) for c in range(1, CHUNKS)]
        pre = [psum.tile([P, len(tiles), CHUNK], F32, name=f"pre{b}", tag=f"pre{b}") for b, (c, tiles) in enumerate(banks)]
        for z in range(PASSES):
            for b, (c, tiles) in enumerate(banks):
                u, within = divmod(c * CHUNK, GATHER)
                for t in tiles:
                    nc.tensor.matmul_mx(
                        out=pre[b][:, t - tiles[0], :],
                        lhsT=w1_codes[z][:, t * P : (t + 1) * P].bitcast(FP8X4),
                        lhsT_scale=w1_scales[z][:, t * P : (t + 1) * P],
                        rhs=picked[z, u][:, within : within + CHUNK].bitcast(FP8X4),
                        rhs_scale=x_planes[z][4 * z : P, c * CHUNK : (c + 1) * CHUNK],
                        start=z == 0 and t == tiles[0],
                        stop=z == PASSES - 1 and t == tiles[-1],
                    )

        acc = {}

        def second_layer(i):
            first, width = PIECES[i]
            c, within = divmod(first, CHUNK)
            hidden = keep.tile([P, width, PACK], BF16, name=f"hidden{i}", tag=f"hidden{i}", align_bytes=ALIGN)
            if c == 0:
                by_tile = keep.tile([P, PACK, CHUNK], BF16, name="by_tile", align_bytes=ALIGN)
                for b, tiles in enumerate(FIRST_BANKS):
                    nc.scalar.activation(by_tile[:, tiles[0] : tiles[-1] + 1, :], pre[b][:], GELU, bias=zero[:, 1:2])
                nc.vector.tensor_copy(
                    hidden[:].rearrange("p (c i) t -> p c t i", i=4), by_tile[:].rearrange("p t (c i) -> p c t i", i=4)
                )
            else:
                bank = pre[len(FIRST_BANKS) - 1 + c]
                nc.scalar.activation(
                    hidden[:], bank[:, :, within : within + width].rearrange("p t n -> p n t"), GELU, bias=zero[:, 1:2]
                )
            h_codes = keep.tile([P, width], U32, name=f"h_codes{i}", align_bytes=ALIGN)
            h_scales = keep.tile([P, width], U8, name=f"h_scales{i}", align_bytes=ALIGN)
            nc.vector.quantize_mx(out=h_codes[:].bitcast(FP8X4), scales=h_scales[:], in_=hidden[:].rearrange("p n t -> p (n t)"))
            acc[i] = psum.tile([P, width], F32, name=f"acc{i}", tag=f"acc{i}" if i < FREE_BANKS else f"pre{i - FREE_BANKS}")
            nc.tensor.matmul_mx(
                out=acc[i][:],
                lhsT=w2_codes[:].bitcast(FP8X4),
                lhsT_scale=w2_scales[:],
                rhs=h_codes[:].bitcast(FP8X4),
                rhs_scale=h_scales[:],
                start=True,
                stop=True,
            )

        second_layer(0)
        second_layer(1)
        half = CHUNK // 2
        for i in range(2, 5):
            second_layer(i)
        early = keep.tile([P, 2 * CHUNK], F32, name="early", align_bytes=ALIGN)
        nc.scalar.copy(early[:, 0:CHUNK], acc[0][:])
        nc.scalar.copy(early[:, CHUNK : 2 * CHUNK], acc[1][:])
        nc.sync.dma_start(out[:, 0 : 2 * CHUNK], early[:])
        late = keep.tile([P, CHUNK + half], F32, name="late", align_bytes=ALIGN)
        nc.scalar.copy(late[:, 0:CHUNK], acc[2][:])
        nc.scalar.copy(late[:, CHUNK : CHUNK + half], acc[3][:])
        nc.sync.dma_start(out[:, 2 * CHUNK : S - half], late[:])
        last = keep.tile([P, half], F32, name="last", align_bytes=ALIGN)
        nc.vector.tensor_copy(last[:], acc[4][:])
        nc.sync.dma_start(out[:, S - half : S], last[:])
